import numpy as np, ml_dtypes
CORES = [36,164,52,180,100,228,116,244]
N = 8
import mx_ref
NC = 512
M = NC // N
BF = ml_dtypes.bfloat16
def cut(t, i, w=512):
    return t[:, w * i:w * i + w]
def term(a, B):
    return np.stack([mx_ref.matmul(mx_ref.quantize(cut(a, i)), B) for i in range(4)], axis=2).reshape(128, -1)
def setup_inputs(rng):
    def f(*shape):
        return mx_ref.flush((rng.standard_normal(shape, dtype=np.float32) * np.exp2(rng.integers(-2, 3, shape[:-1] + (1,)))).astype(BF))
    return {"a": f(N, 128, 4 * 512), "b": f(N, 128, 4 * NC)}
def setup_inputs_blocks(rng):
    d = setup_inputs(rng)
    for k in ("a", "b"): d[k] = mx_ref.spread(d[k], rng, 2)
    return d
def setup_inputs_wide(rng):
    d = setup_inputs(rng)
    for k in ("a", "b"): d[k] = mx_ref.flush((d[k].astype(np.float32) * np.exp2(rng.integers(-4, 5, (N, 1, 1))).astype(np.float32)).astype(BF))
    return d
def setup_inputs_lossless(rng):
    a = np.zeros((N, 128, 4 * 128, 4), np.float32)
    for r in range(N):
        k = rng.integers(0, 512, size=4 * 128)
        a[r, k // 4, np.arange(4 * 128), k % 4] = 1.0
    size = np.repeat(2.0 ** rng.integers(-4, 5, size=(1, 1, (4 * NC) // 4)), 4, axis=2)
    b = rng.integers(-1, 2, size=(N, 128, 4 * NC)) * size
    return {"a": a.reshape(N, 128, 4 * 512).astype(BF), "b": b.astype(np.float32).astype(BF)}
def reference(a, b):
    T = [term(a[r], mx_ref.quantize(b[r])) for r in range(N)]
    y = np.zeros((N, 128, 4 * M), np.float32)
    for c in range(N):
        y[c] = mx_ref.total([cut(T[r], c, 4 * M) for r in range(N)])
    return {"y": y}

@@ -1,0 +1,221 @@
+from concourse.bass import DstId, RemoteDMATransfer
+from concourse.mybir import dt, AluOpType, ActivationFunctionType
+
+N = 8
+WORLD = 256
+PC = 64
+CH = 2 * PC
+OFFS = (1, 2, 3, 0)
+OWN = 3 * CH + PC
+
+SCRATCH = {
+    "a_sb": ("sbuf", [128, 2048], "bfloat16"),
+    "b_sb": ("sbuf", [128, 2048], "bfloat16"),
+    "aq": ("sbuf", [128, 512], "float8_e4m3fn_x4"), "asc": ("sbuf", [128, 512], "uint8"),
+    "bq": ("sbuf", [128, 512], "float8_e4m3fn_x4"), "bsc": ("sbuf", [128, 512], "uint8"),
+    "h": ("sbuf", [128, 2048], "bfloat16"),
+    "hq": ("sbuf", [128, 640], "float8_e4m3fn_x4"), "hsc": ("sbuf", [128, 640], "uint8"),
+    "lq": ("sbuf", [128, 384], "float8_e4m3fn_x4"), "lsc": ("sbuf", [128, 384], "uint8"),
+    "e_sb": ("sbuf", [128, 2048], "bfloat16"),
+    "eq": ("sbuf", [128, 512], "float8_e4m3fn_x4"), "esc": ("sbuf", [128, 512], "uint8"),
+    "fq": ("sbuf", [128, 128], "float8_e4m3fn_x4"), "fsc": ("sbuf", [128, 128], "uint8"),
+    "tmp": ("sbuf", [128, 256], "float32"),
+    "y_sb": ("sbuf", [128, 256], "float32"),
+    "ps": ("psum", [128, 4096], "float32"),
+}
+SEMAPHORES = (["la", "aqs", "e0", "e1", "e2", "sent", "fs", "fc", "yd", "st"]
+              + ["lb%d" % k for k in range(4)] + ["bqs%d" % k for k in range(4)]
+              + ["m%d_%d" % (k, i) for k in range(4) for i in range(4)]
+              + ["ev%d" % k for k in range(4)] + ["hqs%d" % k for k in range(4)]
+              + ["arr%d" % k for k in range(4)] + ["d%d" % t for t in range(4)] + ["c%d" % t for t in range(4)])
+
+
+def _eng(topo, src, dst):
+    m = topo.mask(src, dst)
+    return [i for i in range(m.bit_length()) if (m >> i) & 1]
+
+
+def _helpers(topo, cores, r):
+    me = cores[r]
+    peers = [c for c in range(WORLD) if c != me and topo.host(c) == topo.host(me) and topo.chip(c) == topo.chip(me)
+             and all(topo.may_write(c, d) for d in cores if d != me)]
+    far = [c for c in peers if topo.die(c) != topo.die(me)]
+    near = [c for c in peers if topo.die(c) == topo.die(me)]
+    return far[0], far[1], near[0]
+
+
+def _route(topo, cores, r, k):
+    p = (r // 2 + OFFS[k]) % 4
+    hs = _helpers(topo, cores, r)
+    out = []
+    for d in (2 * p, 2 * p + 1):
+        if d == r:
+            continue
+        if k < 2:
+            e = _eng(topo, hs[k], cores[d])
+            half = len(e) // 2
+            out.append((d, hs[k], e[half * (d % 2):half * (d % 2) + half]))
+        elif k == 2 and d % 2:
+            out.append((d, hs[2], _eng(topo, hs[2], cores[d])))
+        else:
+            out.append((d, None, _eng(topo, cores[r], cores[d])))
+    return out
+
+
+def _land(r, d, k):
+    if k < 3:
+        return "lq", "lsc", CH * k + PC * (r % 2)
+    return "hq", "hsc", (OWN - PC if d % 2 == 0 else OWN + CH)
+
+
+def rank_program(g, core, T, topo):
+    cores = list(T.cores)
+    S = T.sem
+    sent = [0]
+
+    def push(items):
+        for which in (1, 0):
+            tr = []
+            for (dc, sb, s0, db, d0, n, sems, eng) in items:
+                rid, pid = topo.addr(dc, core)
+                src, dst = T[sb[which]][:, s0:s0 + n], T[db[which]][:, d0:d0 + n]
+                if which == 0:
+                    src, dst = src.bitcast(dt.uint8), dst.bitcast(dt.uint8)
+                tr.append(RemoteDMATransfer(dst_ids=[DstId(rid=rid, pnc=pid)], dma_engine_mask=sum(1 << i for i in eng),
+                                            remote_sem=sems[1 - which], src=src, dst=dst))
+                sent[0] += len(eng)
+            yield tr
+
+    rank = T.rank_of(core)
+    if rank is None:
+        for r in range(N):
+            hs = _helpers(topo, cores, r)
+            if core not in hs:
+                continue
+            k = hs.index(core)
+            mine = [x for x in _route(topo, cores, r, k) if x[1] == core]
+            n_in = len(_eng(topo, cores[r], core)) if k < 2 else len(_eng(topo, cores[r], core)) - len(_eng(topo, cores[r], cores[mine[0][0]]))
+            items = []
+            for (d, via, eng) in mine:
+                lb = _land(r, d, k)
+                items.append((cores[d], ("fq", "fsc"), (PC * (d % 2) if k < 2 else 0), (lb[0], lb[1]), lb[2], PC,
+                              (S["arr%d" % k], S["arr%d" % k]), eng))
+            for sem, tr in zip((S.fs, S.fc), push(items)):
+                g.wait_ge(sem, n_in)
+                g.remote_dma_fused(tr, local_sem=S.sent)
+            g.wait_ge(S.sent, sent[0])
+        return
+
+    r = rank
+    v, s, te, sy = g.vector, g.scalar, g.tensor, g.sync
+    pair = [(r // 2 + OFFS[k]) % 4 for k in range(4)]
+    hcol = [0, CH, 2 * CH, OWN]
+
+    sy.dma_start(T.a_sb[:], T.a[:]).then_inc(S.la, 16)
+    for k in range(4):
+        c0 = 4 * CH * pair[k]
+        s.dma_start(T.b_sb[:, c0:c0 + 4 * CH], T.b[:, c0:c0 + 4 * CH]).then_inc(S["lb%d" % k], 16)
+
+    def quant_b(k):
+        p = pair[k]
+        v.wait_ge(S["lb%d" % k], 16)
+        v.quantize_mx(T.bq[:, CH * p:CH * p + CH], T.bsc[:, CH * p:CH * p + CH],
+                      T.b_sb[:, 4 * CH * p:4 * CH * p + 4 * CH]).then_inc(S["bqs%d" % k], 1)
+
+    def bank(k, i):
+        b = 512 * (4 * (k % 2) + i)
+        return T.ps[:, b:b + CH]
+
+    v.memset(T.e_sb[:], 1.0).then_inc(S.e0, 1)
+    v.wait_ge(S.la, 16)
+    v.quantize_mx(T.aq[:], T.asc[:], T.a_sb[:]).then_inc(S.aqs, 1)
+    quant_b(0)
+    for k in range(4):
+        v.wait_ge(S["m%d_0" % k], 1)
+        v.tensor_copy(T.h[:, 512 * k:512 * k + 512:4], bank(k, 0)).then_inc(S["ev%d" % k], 1)
+        if k < 3:
+            quant_b(k + 1)
+        v.wait_ge(S["ev%d" % k], 4)
+        v.quantize_mx(T.hq[:, hcol[k]:hcol[k] + CH], T.hsc[:, hcol[k]:hcol[k] + CH],
+                      T.h[:, 512 * k:512 * k + 512]).then_inc(S["hqs%d" % k], 1)
+    v.wait_ge(S.e1, 1)
+    v.quantize_mx(T.eq[:], T.esc[:], T.e_sb[:]).then_inc(S.e2, 1)
+
+    for k in range(4):
+        for i in (1, 2, 3):
+            s.wait_ge(S["m%d_%d" % (k, i)], 1)
+            s.activation(T.h[:, 512 * k + i:512 * k + 512:4], bank(k, i), ActivationFunctionType.Copy).then_inc(S["ev%d" % k], 1)
+
+    te.wait_ge(S.aqs, 1)
+    for k in range(4):
+        p = pair[k]
+        te.wait_ge(S["bqs%d" % k], 1)
+        if k >= 2:
+            te.wait_ge(S["ev%d" % (k - 2)], 4)
+        for i in range(4):
+            te.matmul_mx(bank(k, i), T.aq[:, 128 * i:128 * i + 128], T.asc[:, 128 * i:128 * i + 128],
+                         T.bq[:, CH * p:CH * p + CH], T.bsc[:, CH * p:CH * p + CH], True, True).then_inc(S["m%d_%d" % (k, i)], 1)
+
+    g.wait_ge(S.e0, 1)
+    g.affine_select(T.e_sb[:], T.e_sb[:], [[1, 4], [-1, 512]], AluOpType.is_equal, 0.0, 0, 4).then_inc(S.e1, 1)
+    for k in range(4):
+        rt = _route(topo, cores, r, k)
+        items = []
+        if k < 2:
+            hc = rt[0][1]
+            items.append((hc, ("hq", "hsc"), hcol[k], ("fq", "fsc"), 0, CH, (S.fs, S.fc), _eng(topo, core, hc)))
+        else:
+            away = []
+            for (d, via, eng) in rt:
+                if via is None:
+                    lb = _land(r, d, k)
+                    away = eng
+                    items.append((cores[d], ("hq", "hsc"), hcol[k] + PC * (d % 2), (lb[0], lb[1]), lb[2], PC,
+                                  (S["arr%d" % k], S["arr%d" % k]), eng))
+            for (d, via, eng) in rt:
+                if via is not None:
+                    rest = [i for i in _eng(topo, core, via) if i not in away]
+                    items.append((via, ("hq", "hsc"), hcol[k] + PC * (d % 2), ("fq", "fsc"), 0, PC, (S.fs, S.fc), rest))
+        g.wait_ge(S["hqs%d" % k], 1)
+        for tr in push(items):
+            g.remote_dma_fused(tr, local_sem=S.sent)
+    g.wait_ge(S.sent, sent[0])
+
+    need = [0, 0, 0, 0]
+    for q in range(N):
+        if q == r:
+            continue
+        for k in range(4):
+            for (d, via, eng) in _route(topo, cores, q, k):
+                if d == r:
+                    need[k] += 2 * len(eng)
+    order = (2, 3, 0, 1) if r % 2 == 0 else (3, 0, 1, 2)
+    te.wait_ge(S.e2, 1)
+    te.wait_ge(S.ev2, 4)
+    for n_, k in enumerate(order):
+        te.wait_ge(S["arr%d" % k], need[k])
+        if k < 3:
+            wq, ws = T.lq[:, CH * k:CH * k + CH], T.lsc[:, CH * k:CH * k + CH]
+        else:
+            te.wait_ge(S.hqs3, 1)
+            w0 = OWN - PC if r % 2 == 0 else OWN + PC
+            wq, ws = T.hq[:, w0:w0 + CH], T.hsc[:, w0:w0 + CH]
+        for t in range(4):
+            mm = te.matmul_mx(T.ps[:, 512 * t:512 * t + CH], T.eq[:, 128 * t:128 * t + 128], T.esc[:, 128 * t:128 * t + 128],
+                              wq, ws, n_ == 0, n_ == 3)
+            if n_ == 3:
+                mm.then_inc(S["d%d" % t], 1)
+
+    for t in (2, 3):
+        s.wait_ge(S["d%d" % t], 1)
+        s.activation(T.tmp[:, PC * t:PC * t + PC], T.ps[:, 512 * t:512 * t + PC], ActivationFunctionType.Copy).then_inc(S["c%d" % t], 1)
+    for t in (0, 1):
+        v.wait_ge(S["d%d" % t], 1)
+        v.tensor_copy(T.tmp[:, PC * t:PC * t + PC], T.ps[:, 512 * t:512 * t + PC]).then_inc(S["c%d" % t], 1)
+    for t in range(4):
+        v.wait_ge(S["d%d" % t], 1)
+        v.wait_ge(S["c%d" % t], 1)
+        v.tensor_tensor(T.y_sb[:, t:256:4], T.ps[:, 512 * t + PC:512 * t + CH], T.tmp[:, PC * t:PC * t + PC], AluOpType.add).then_inc(S.yd, 1)
+    sy.wait_ge(S.yd, 4)
+    sy.dma_start(T.y[:], T.y_sb[:]).then_inc(S.st, 16)
+    sy.wait_ge(S.st, 16)

@@ -7,6 +7,8 @@ PC = 64
 CH = 2 * PC
 OFFS = (1, 2, 3, 0)
 OWN = 3 * CH + PC
+PLAN = ((0, 1), (2, 3), (None, None), (None, None))
+ORDER = ((2, 0, 3, 1), (2, 0, 3, 1))
 
 SCRATCH = {
     "a_sb": ("sbuf", [128, 2048], "bfloat16"),
@@ -16,6 +18,7 @@ SCRATCH = {
     "h": ("sbuf", [128, 2048], "bfloat16"),
     "hq": ("sbuf", [128, 640], "float8_e4m3fn_x4"), "hsc": ("sbuf", [128, 640], "uint8"),
     "lq": ("sbuf", [128, 384], "float8_e4m3fn_x4"), "lsc": ("sbuf", [128, 384], "uint8"),
+    "g_sb": ("sbuf", [128, 520], "bfloat16"),
     "e_sb": ("sbuf", [128, 2048], "bfloat16"),
     "eq": ("sbuf", [128, 512], "float8_e4m3fn_x4"), "esc": ("sbuf", [128, 512], "uint8"),
     "fq": ("sbuf", [128, 128], "float8_e4m3fn_x4"), "fsc": ("sbuf", [128, 128], "uint8"),
@@ -23,7 +26,8 @@ SCRATCH = {
     "y_sb": ("sbuf", [128, 256], "float32"),
     "ps": ("psum", [128, 4096], "float32"),
 }
-SEMAPHORES = (["la", "aqs", "e0", "e1", "e2", "sent", "fs", "fc", "yd", "st"]
+SEMAPHORES = (["la", "e0", "e1", "e2", "e3", "sent", "fs", "fc", "yd", "st"]
+              + ["aqs%d" % i for i in range(4)]
               + ["lb%d" % k for k in range(4)] + ["bqs%d" % k for k in range(4)]
               + ["m%d_%d" % (k, i) for k in range(4) for i in range(4)]
               + ["ev%d" % k for k in range(4)] + ["hqs%d" % k for k in range(4)]
@@ -39,26 +43,41 @@ def _helpers(topo, cores, r):
     me = cores[r]
     peers = [c for c in range(WORLD) if c != me and topo.host(c) == topo.host(me) and topo.chip(c) == topo.chip(me)
              and all(topo.may_write(c, d) for d in cores if d != me)]
-    far = [c for c in peers if topo.die(c) != topo.die(me)]
-    near = [c for c in peers if topo.die(c) == topo.die(me)]
-    return far[0], far[1], near[0]
+    return [c for c in peers if topo.die(c) != topo.die(me)] + [c for c in peers if topo.die(c) == topo.die(me)]
 
 
-def _route(topo, cores, r, k):
+def _step(topo, cores, r, k):
     p = (r // 2 + OFFS[k]) % 4
-    hs = _helpers(topo, cores, r)
+    me = cores[r]
+    ds = [d for d in (2 * p, 2 * p + 1) if d != r]
+    direct = [d for d in ds if PLAN[k][d % 2] is None]
+    fw = {}
+    for d in ds:
+        if PLAN[k][d % 2] is not None:
+            fw.setdefault(PLAN[k][d % 2], []).append(d)
     out = []
-    for d in (2 * p, 2 * p + 1):
-        if d == r:
-            continue
-        if k < 2:
-            e = _eng(topo, hs[k], cores[d])
-            half = len(e) // 2
-            out.append((d, hs[k], e[half * (d % 2):half * (d % 2) + half]))
-        elif k == 2 and d % 2:
-            out.append((d, hs[2], _eng(topo, hs[2], cores[d])))
+    lo = _eng(topo, me, cores[ds[0]])
+    for j, d in enumerate(direct):
+        w = len(lo) // len(direct)
+        out.append((cores[d], [d], lo[j * w:j * w + w], True))
+    hs = _helpers(topo, cores, r) if fw else []
+    for j, h in enumerate(sorted(fw)):
+        al = [i for i in _eng(topo, me, hs[h]) if not (direct and i in lo)]
+        w = len(al) // len(fw)
+        out.append((hs[h], fw[h], al[j * w:j * w + w], False))
+    return out
+
+
+def _last(topo, cores, r, k):
+    out = []
+    for (tc, dl, eng, straight) in _step(topo, cores, r, k):
+        if straight:
+            out.append((cores[r], dl[0], eng))
         else:
-            out.append((d, None, _eng(topo, cores[r], cores[d])))
+            for j, d in enumerate(dl):
+                e = _eng(topo, tc, cores[d])
+                w = len(e) // len(dl)
+                out.append((tc, d, e[j * w:j * w + w]))
     return out
 
 
@@ -89,21 +108,22 @@ def rank_program(g, core, T, topo):
     rank = T.rank_of(core)
     if rank is None:
         for r in range(N):
-            hs = _helpers(topo, cores, r)
-            if core not in hs:
+            if topo.host(cores[r]) != topo.host(core) or topo.chip(cores[r]) != topo.chip(core):
                 continue
-            k = hs.index(core)
-            mine = [x for x in _route(topo, cores, r, k) if x[1] == core]
-            n_in = len(_eng(topo, cores[r], core)) if k < 2 else len(_eng(topo, cores[r], core)) - len(_eng(topo, cores[r], cores[mine[0][0]]))
-            items = []
-            for (d, via, eng) in mine:
-                lb = _land(r, d, k)
-                items.append((cores[d], ("fq", "fsc"), (PC * (d % 2) if k < 2 else 0), (lb[0], lb[1]), lb[2], PC,
-                              (S["arr%d" % k], S["arr%d" % k]), eng))
-            for sem, tr in zip((S.fs, S.fc), push(items)):
-                g.wait_ge(sem, n_in)
-                g.remote_dma_fused(tr, local_sem=S.sent)
-            g.wait_ge(S.sent, sent[0])
+            for k in range(4):
+                for (tc, dl, eng_in, straight) in _step(topo, cores, r, k):
+                    if tc != core or straight:
+                        continue
+                    items = []
+                    for (sc, d, eng) in _last(topo, cores, r, k):
+                        if sc == core:
+                            lb = _land(r, d, k)
+                            items.append((cores[d], ("fq", "fsc"), PC * dl.index(d), (lb[0], lb[1]), lb[2], PC,
+                                          (S["arr%d" % k], S["arr%d" % k]), eng))
+                    for sem, tr in zip((S.fs, S.fc), push(items)):
+                        g.wait_ge(sem, len(eng_in))
+                        g.remote_dma_fused(tr, local_sem=S.sent)
+                    g.wait_ge(S.sent, sent[0])
         return
 
     r = rank
@@ -111,10 +131,14 @@ def rank_program(g, core, T, topo):
     pair = [(r // 2 + OFFS[k]) % 4 for k in range(4)]
     hcol = [0, CH, 2 * CH, OWN]
 
-    sy.dma_start(T.a_sb[:], T.a[:]).then_inc(S.la, 16)
-    for k in range(4):
+    def load_b(q, k):
         c0 = 4 * CH * pair[k]
-        s.dma_start(T.b_sb[:, c0:c0 + 4 * CH], T.b[:, c0:c0 + 4 * CH]).then_inc(S["lb%d" % k], 16)
+        q.dma_start(T.b_sb[:, c0:c0 + 4 * CH], T.b[:, c0:c0 + 4 * CH]).then_inc(S["lb%d" % k], 16)
+
+    load_b(s, 0)
+    sy.dma_start(T.a_sb[:], T.a[:]).then_inc(S.la, 16)
+    for k in (1, 2, 3):
+        load_b(sy, k)
 
     def quant_b(k):
         p = pair[k]
@@ -126,10 +150,12 @@ def rank_program(g, core, T, topo):
         b = 512 * (4 * (k % 2) + i)
         return T.ps[:, b:b + CH]
 
-    v.memset(T.e_sb[:], 1.0).then_inc(S.e0, 1)
-    v.wait_ge(S.la, 16)
-    v.quantize_mx(T.aq[:], T.asc[:], T.a_sb[:]).then_inc(S.aqs, 1)
+    v.memset(T.g_sb[:], 1.0).then_inc(S.e0, 1)
     quant_b(0)
+    v.wait_ge(S.la, 16)
+    for i in range(4):
+        v.quantize_mx(T.aq[:, 128 * i:128 * i + 128], T.asc[:, 128 * i:128 * i + 128],
+                      T.a_sb[:, 512 * i:512 * i + 512]).then_inc(S["aqs%d" % i], 1)
     for k in range(4):
         v.wait_ge(S["m%d_0" % k], 1)
         v.tensor_copy(T.h[:, 512 * k:512 * k + 512:4], bank(k, 0)).then_inc(S["ev%d" % k], 1)
@@ -139,43 +165,41 @@ def rank_program(g, core, T, topo):
         v.quantize_mx(T.hq[:, hcol[k]:hcol[k] + CH], T.hsc[:, hcol[k]:hcol[k] + CH],
                       T.h[:, 512 * k:512 * k + 512]).then_inc(S["hqs%d" % k], 1)
     v.wait_ge(S.e1, 1)
+    for t in (0, 1):
+        v.tensor_copy(T.e_sb[:, 512 * t:512 * t + 512], T.g_sb[:, 4 - t:4 - t + 512]).then_inc(S.e3, 1)
+    v.wait_ge(S.e3, 4)
     v.quantize_mx(T.eq[:], T.esc[:], T.e_sb[:]).then_inc(S.e2, 1)
 
+    s.wait_ge(S.e1, 1)
+    for t in (2, 3):
+        s.activation(T.e_sb[:, 512 * t:512 * t + 512], T.g_sb[:, 4 - t:4 - t + 512], ActivationFunctionType.Copy).then_inc(S.e3, 1)
     for k in range(4):
         for i in (1, 2, 3):
             s.wait_ge(S["m%d_%d" % (k, i)], 1)
             s.activation(T.h[:, 512 * k + i:512 * k + 512:4], bank(k, i), ActivationFunctionType.Copy).then_inc(S["ev%d" % k], 1)
 
-    te.wait_ge(S.aqs, 1)
     for k in range(4):
         p = pair[k]
         te.wait_ge(S["bqs%d" % k], 1)
         if k >= 2:
             te.wait_ge(S["ev%d" % (k - 2)], 4)
         for i in range(4):
+            if k == 0:
+                te.wait_ge(S["aqs%d" % i], 1)
             te.matmul_mx(bank(k, i), T.aq[:, 128 * i:128 * i + 128], T.asc[:, 128 * i:128 * i + 128],
                          T.bq[:, CH * p:CH * p + CH], T.bsc[:, CH * p:CH * p + CH], True, True).then_inc(S["m%d_%d" % (k, i)], 1)
 
     g.wait_ge(S.e0, 1)
-    g.affine_select(T.e_sb[:], T.e_sb[:], [[1, 4], [-1, 512]], AluOpType.is_equal, 0.0, 0, 4).then_inc(S.e1, 1)
+    g.affine_select(T.g_sb[:], T.g_sb[:], [[-1, 520]], AluOpType.is_equal, 0.0, 4, 4).then_inc(S.e1, 1)
     for k in range(4):
-        rt = _route(topo, cores, r, k)
         items = []
-        if k < 2:
-            hc = rt[0][1]
-            items.append((hc, ("hq", "hsc"), hcol[k], ("fq", "fsc"), 0, CH, (S.fs, S.fc), _eng(topo, core, hc)))
-        else:
-            away = []
-            for (d, via, eng) in rt:
-                if via is None:
-                    lb = _land(r, d, k)
-                    away = eng
-                    items.append((cores[d], ("hq", "hsc"), hcol[k] + PC * (d % 2), (lb[0], lb[1]), lb[2], PC,
-                                  (S["arr%d" % k], S["arr%d" % k]), eng))
-            for (d, via, eng) in rt:
-                if via is not None:
-                    rest = [i for i in _eng(topo, core, via) if i not in away]
-                    items.append((via, ("hq", "hsc"), hcol[k] + PC * (d % 2), ("fq", "fsc"), 0, PC, (S.fs, S.fc), rest))
+        for (tc, dl, eng, straight) in _step(topo, cores, r, k):
+            c0 = hcol[k] + PC * (dl[0] % 2)
+            if straight:
+                lb = _land(r, dl[0], k)
+                items.append((tc, ("hq", "hsc"), c0, (lb[0], lb[1]), lb[2], PC, (S["arr%d" % k], S["arr%d" % k]), eng))
+            else:
+                items.append((tc, ("hq", "hsc"), c0, ("fq", "fsc"), 0, PC * len(dl), (S.fs, S.fc), eng))
         g.wait_ge(S["hqs%d" % k], 1)
         for tr in push(items):
             g.remote_dma_fused(tr, local_sem=S.sent)
@@ -183,16 +207,13 @@ def rank_program(g, core, T, topo):
 
     need = [0, 0, 0, 0]
     for q in range(N):
-        if q == r:
-            continue
         for k in range(4):
-            for (d, via, eng) in _route(topo, cores, q, k):
+            for (sc, d, eng) in _last(topo, cores, q, k):
                 if d == r:
                     need[k] += 2 * len(eng)
-    order = (2, 3, 0, 1) if r % 2 == 0 else (3, 0, 1, 2)
     te.wait_ge(S.e2, 1)
     te.wait_ge(S.ev2, 4)
-    for n_, k in enumerate(order):
+    for n_, k in enumerate(ORDER[r % 2]):
         te.wait_ge(S["arr%d" % k], need[k])
         if k < 3:
             wq, ws = T.lq[:, CH * k:CH * k + CH], T.lsc[:, CH * k:CH * k + CH]

@@ -7,8 +7,8 @@ PC = 64
 CH = 2 * PC
 OFFS = (1, 2, 3, 0)
 OWN = 3 * CH + PC
-PLAN = ((0, 1), (2, 3), (None, None), (None, None))
-ORDER = ((2, 0, 3, 1), (2, 0, 3, 1))
+PLAN = ((0, 1), (None, 0), (1, None), (None, None))
+ORDER = ((1, 3, 0, 2), (2, 3, 0, 1))
 
 SCRATCH = {
     "a_sb": ("sbuf", [128, 2048], "bfloat16"),
@@ -19,15 +19,14 @@ SCRATCH = {
     "hq": ("sbuf", [128, 640], "float8_e4m3fn_x4"), "hsc": ("sbuf", [128, 640], "uint8"),
     "lq": ("sbuf", [128, 384], "float8_e4m3fn_x4"), "lsc": ("sbuf", [128, 384], "uint8"),
     "g_sb": ("sbuf", [128, 520], "bfloat16"),
-    "e_sb": ("sbuf", [128, 2048], "bfloat16"),
     "eq": ("sbuf", [128, 512], "float8_e4m3fn_x4"), "esc": ("sbuf", [128, 512], "uint8"),
     "fq": ("sbuf", [128, 128], "float8_e4m3fn_x4"), "fsc": ("sbuf", [128, 128], "uint8"),
     "tmp": ("sbuf", [128, 256], "float32"),
     "y_sb": ("sbuf", [128, 256], "float32"),
     "ps": ("psum", [128, 4096], "float32"),
 }
-SEMAPHORES = (["la", "e0", "e1", "e2", "e3", "sent", "fs", "fc", "yd", "st"]
-              + ["aqs%d" % i for i in range(4)]
+SEMAPHORES = (["la0", "la1", "e0", "e1", "sent", "fs0", "fc0", "fs1", "fc1", "yd", "st"]
+              + ["aqs%d" % i for i in range(4)] + ["pk%d" % t for t in range(4)]
               + ["lb%d" % k for k in range(4)] + ["bqs%d" % k for k in range(4)]
               + ["m%d_%d" % (k, i) for k in range(4) for i in range(4)]
               + ["ev%d" % k for k in range(4)] + ["hqs%d" % k for k in range(4)]
@@ -62,10 +61,14 @@ def _step(topo, cores, r, k):
         out.append((cores[d], [d], lo[j * w:j * w + w], True))
     hs = _helpers(topo, cores, r) if fw else []
     for j, h in enumerate(sorted(fw)):
-        al = [i for i in _eng(topo, me, hs[h]) if not (direct and i in lo)]
+        al = [i for i in _eng(topo, me, hs[h]) if i not in lo]
         w = len(al) // len(fw)
         out.append((hs[h], fw[h], al[j * w:j * w + w], False))
     return out
+
+
+def _slot(k, h):
+    return sum(1 for q in range(k) if h in PLAN[q])
 
 
 def _last(topo, cores, r, k):
@@ -110,20 +113,23 @@ def rank_program(g, core, T, topo):
         for r in range(N):
             if topo.host(cores[r]) != topo.host(core) or topo.chip(cores[r]) != topo.chip(core):
                 continue
+            hs = _helpers(topo, cores, r)
             for k in range(4):
                 for (tc, dl, eng_in, straight) in _step(topo, cores, r, k):
                     if tc != core or straight:
                         continue
+                    sl = _slot(k, hs.index(core))
                     items = []
                     for (sc, d, eng) in _last(topo, cores, r, k):
                         if sc == core:
                             lb = _land(r, d, k)
-                            items.append((cores[d], ("fq", "fsc"), PC * dl.index(d), (lb[0], lb[1]), lb[2], PC,
+                            items.append((cores[d], ("fq", "fsc"), PC * sl, (lb[0], lb[1]), lb[2], PC,
                                           (S["arr%d" % k], S["arr%d" % k]), eng))
-                    for sem, tr in zip((S.fs, S.fc), push(items)):
+                    for sem, tr in zip((S["fs%d" % sl], S["fc%d" % sl]), push(items)):
                         g.wait_ge(sem, len(eng_in))
                         g.remote_dma_fused(tr, local_sem=S.sent)
-                    g.wait_ge(S.sent, sent[0])
+            if sent[0]:
+                g.wait_ge(S.sent, sent[0])
         return
 
     r = rank
@@ -136,7 +142,8 @@ def rank_program(g, core, T, topo):
         q.dma_start(T.b_sb[:, c0:c0 + 4 * CH], T.b[:, c0:c0 + 4 * CH]).then_inc(S["lb%d" % k], 16)
 
     load_b(s, 0)
-    sy.dma_start(T.a_sb[:], T.a[:]).then_inc(S.la, 16)
+    for hf in (0, 1):
+        sy.dma_start(T.a_sb[:, 1024 * hf:1024 * hf + 1024], T.a[:, 1024 * hf:1024 * hf + 1024]).then_inc(S["la%d" % hf], 16)
     for k in (1, 2, 3):
         load_b(sy, k)
 
@@ -152,8 +159,9 @@ def rank_program(g, core, T, topo):
 
     v.memset(T.g_sb[:], 1.0).then_inc(S.e0, 1)
     quant_b(0)
-    v.wait_ge(S.la, 16)
     for i in range(4):
+        if i % 2 == 0:
+            v.wait_ge(S["la%d" % (i // 2)], 16)
         v.quantize_mx(T.aq[:, 128 * i:128 * i + 128], T.asc[:, 128 * i:128 * i + 128],
                       T.a_sb[:, 512 * i:512 * i + 512]).then_inc(S["aqs%d" % i], 1)
     for k in range(4):
@@ -165,14 +173,10 @@ def rank_program(g, core, T, topo):
         v.quantize_mx(T.hq[:, hcol[k]:hcol[k] + CH], T.hsc[:, hcol[k]:hcol[k] + CH],
                       T.h[:, 512 * k:512 * k + 512]).then_inc(S["hqs%d" % k], 1)
     v.wait_ge(S.e1, 1)
-    for t in (0, 1):
-        v.tensor_copy(T.e_sb[:, 512 * t:512 * t + 512], T.g_sb[:, 4 - t:4 - t + 512]).then_inc(S.e3, 1)
-    v.wait_ge(S.e3, 4)
-    v.quantize_mx(T.eq[:], T.esc[:], T.e_sb[:]).then_inc(S.e2, 1)
+    for t in range(4):
+        v.quantize_mx(T.eq[:, 128 * t:128 * t + 128], T.esc[:, 128 * t:128 * t + 128],
+                      T.g_sb[:, 4 - t:4 - t + 512]).then_inc(S["pk%d" % t], 1)
 
-    s.wait_ge(S.e1, 1)
-    for t in (2, 3):
-        s.activation(T.e_sb[:, 512 * t:512 * t + 512], T.g_sb[:, 4 - t:4 - t + 512], ActivationFunctionType.Copy).then_inc(S.e3, 1)
     for k in range(4):
         for i in (1, 2, 3):
             s.wait_ge(S["m%d_%d" % (k, i)], 1)
@@ -199,7 +203,8 @@ def rank_program(g, core, T, topo):
                 lb = _land(r, dl[0], k)
                 items.append((tc, ("hq", "hsc"), c0, (lb[0], lb[1]), lb[2], PC, (S["arr%d" % k], S["arr%d" % k]), eng))
             else:
-                items.append((tc, ("hq", "hsc"), c0, ("fq", "fsc"), 0, PC * len(dl), (S.fs, S.fc), eng))
+                sl = _slot(k, PLAN[k][dl[0] % 2])
+                items.append((tc, ("hq", "hsc"), c0, ("fq", "fsc"), PC * sl, PC, (S["fs%d" % sl], S["fc%d" % sl]), eng))
         g.wait_ge(S["hqs%d" % k], 1)
         for tr in push(items):
             g.remote_dma_fused(tr, local_sem=S.sent)
@@ -211,7 +216,6 @@ def rank_program(g, core, T, topo):
             for (sc, d, eng) in _last(topo, cores, q, k):
                 if d == r:
                     need[k] += 2 * len(eng)
-    te.wait_ge(S.e2, 1)
     te.wait_ge(S.ev2, 4)
     for n_, k in enumerate(ORDER[r % 2]):
         te.wait_ge(S["arr%d" % k], need[k])
@@ -222,6 +226,8 @@ def rank_program(g, core, T, topo):
             w0 = OWN - PC if r % 2 == 0 else OWN + PC
             wq, ws = T.hq[:, w0:w0 + CH], T.hsc[:, w0:w0 + CH]
         for t in range(4):
+            if n_ == 0:
+                te.wait_ge(S["pk%d" % t], 1)
             mm = te.matmul_mx(T.ps[:, 512 * t:512 * t + CH], T.eq[:, 128 * t:128 * t + 128], T.esc[:, 128 * t:128 * t + 128],
                               wq, ws, n_ == 0, n_ == 3)
             if n_ == 3:

from concourse.bass import DstId, RemoteDMATransfer
from concourse.mybir import dt, AluOpType, ActivationFunctionType

N = 8
WORLD = 256
PC = 64
CH = 2 * PC
OFFS = (1, 2, 3, 0)
OWN = 3 * CH + PC
PLAN = ((0, 1), (None, 0), (1, None), (None, None))
ORDER = ((1, 3, 0, 2), (2, 3, 0, 1))

SCRATCH = {
    "a_sb": ("sbuf", [128, 2048], "bfloat16"),
    "b_sb": ("sbuf", [128, 2048], "bfloat16"),
    "aq": ("sbuf", [128, 512], "float8_e4m3fn_x4"), "asc": ("sbuf", [128, 512], "uint8"),
    "bq": ("sbuf", [128, 512], "float8_e4m3fn_x4"), "bsc": ("sbuf", [128, 512], "uint8"),
    "h": ("sbuf", [128, 2048], "bfloat16"),
    "hq": ("sbuf", [128, 640], "float8_e4m3fn_x4"), "hsc": ("sbuf", [128, 640], "uint8"),
    "lq": ("sbuf", [128, 384], "float8_e4m3fn_x4"), "lsc": ("sbuf", [128, 384], "uint8"),
    "g_sb": ("sbuf", [128, 520], "bfloat16"),
    "eq": ("sbuf", [128, 512], "float8_e4m3fn_x4"), "esc": ("sbuf", [128, 512], "uint8"),
    "fq": ("sbuf", [128, 128], "float8_e4m3fn_x4"), "fsc": ("sbuf", [128, 128], "uint8"),
    "tmp": ("sbuf", [128, 256], "float32"),
    "y_sb": ("sbuf", [128, 256], "float32"),
    "ps": ("psum", [128, 4096], "float32"),
}
SEMAPHORES = (["la0", "la1", "e0", "e1", "sent", "fs0", "fc0", "fs1", "fc1", "yd", "st"]
              + ["aqs%d" % i for i in range(4)] + ["pk%d" % t for t in range(4)]
              + ["lb%d" % k for k in range(4)] + ["bqs%d" % k for k in range(4)]
              + ["m%d_%d" % (k, i) for k in range(4) for i in range(4)]
              + ["ev%d" % k for k in range(4)] + ["hqs%d" % k for k in range(4)]
              + ["arr%d" % k for k in range(4)] + ["d%d" % t for t in range(4)] + ["c%d" % t for t in range(4)])


def _eng(topo, src, dst):
    m = topo.mask(src, dst)
    return [i for i in range(m.bit_length()) if (m >> i) & 1]


def _helpers(topo, cores, r):
    me = cores[r]
    peers = [c for c in range(WORLD) if c != me and topo.host(c) == topo.host(me) and topo.chip(c) == topo.chip(me)
             and all(topo.may_write(c, d) for d in cores if d != me)]
    return [c for c in peers if topo.die(c) != topo.die(me)] + [c for c in peers if topo.die(c) == topo.die(me)]


def _step(topo, cores, r, k):
    p = (r // 2 + OFFS[k]) % 4
    me = cores[r]
    ds = [d for d in (2 * p, 2 * p + 1) if d != r]
    direct = [d for d in ds if PLAN[k][d % 2] is None]
    fw = {}
    for d in ds:
        if PLAN[k][d % 2] is not None:
            fw.setdefault(PLAN[k][d % 2], []).append(d)
    out = []
    lo = _eng(topo, me, cores[ds[0]])
    for j, d in enumerate(direct):
        w = len(lo) // len(direct)
        out.append((cores[d], [d], lo[j * w:j * w + w], True))
    hs = _helpers(topo, cores, r) if fw else []
    for j, h in enumerate(sorted(fw)):
        al = [i for i in _eng(topo, me, hs[h]) if i not in lo]
        w = len(al) // len(fw)
        out.append((hs[h], fw[h], al[j * w:j * w + w], False))
    return out


def _slot(k, h):
    return sum(1 for q in range(k) if h in PLAN[q])


def _last(topo, cores, r, k):
    out = []
    for (tc, dl, eng, straight) in _step(topo, cores, r, k):
        if straight:
            out.append((cores[r], dl[0], eng))
        else:
            for j, d in enumerate(dl):
                e = _eng(topo, tc, cores[d])
                w = len(e) // len(dl)
                out.append((tc, d, e[j * w:j * w + w]))
    return out


def _land(r, d, k):
    if k < 3:
        return "lq", "lsc", CH * k + PC * (r % 2)
    return "hq", "hsc", (OWN - PC if d % 2 == 0 else OWN + CH)


def rank_program(g, core, T, topo):
    cores = list(T.cores)
    S = T.sem
    sent = [0]

    def push(items):
        for which in (1, 0):
            tr = []
            for (dc, sb, s0, db, d0, n, sems, eng) in items:
                rid, pid = topo.addr(dc, core)
                src, dst = T[sb[which]][:, s0:s0 + n], T[db[which]][:, d0:d0 + n]
                if which == 0:
                    src, dst = src.bitcast(dt.uint8), dst.bitcast(dt.uint8)
                tr.append(RemoteDMATransfer(dst_ids=[DstId(rid=rid, pnc=pid)], dma_engine_mask=sum(1 << i for i in eng),
                                            remote_sem=sems[1 - which], src=src, dst=dst))
                sent[0] += len(eng)
            yield tr

    rank = T.rank_of(core)
    if rank is None:
        for r in range(N):
            if topo.host(cores[r]) != topo.host(core) or topo.chip(cores[r]) != topo.chip(core):
                continue
            hs = _helpers(topo, cores, r)
            for k in range(4):
                for (tc, dl, eng_in, straight) in _step(topo, cores, r, k):
                    if tc != core or straight:
                        continue
                    sl = _slot(k, hs.index(core))
                    items = []
                    for (sc, d, eng) in _last(topo, cores, r, k):
                        if sc == core:
                            lb = _land(r, d, k)
                            items.append((cores[d], ("fq", "fsc"), PC * sl, (lb[0], lb[1]), lb[2], PC,
                                          (S["arr%d" % k], S["arr%d" % k]), eng))
                    for sem, tr in zip((S["fs%d" % sl], S["fc%d" % sl]), push(items)):
                        g.wait_ge(sem, len(eng_in))
                        g.remote_dma_fused(tr, local_sem=S.sent)
            if sent[0]:
                g.wait_ge(S.sent, sent[0])
        return

    r = rank
    v, s, te, sy = g.vector, g.scalar, g.tensor, g.sync
    pair = [(r // 2 + OFFS[k]) % 4 for k in range(4)]
    hcol = [0, CH, 2 * CH, OWN]

    def load_b(q, k):
        c0 = 4 * CH * pair[k]
        q.dma_start(T.b_sb[:, c0:c0 + 4 * CH], T.b[:, c0:c0 + 4 * CH]).then_inc(S["lb%d" % k], 16)

    load_b(s, 0)
    for hf in (0, 1):
        sy.dma_start(T.a_sb[:, 1024 * hf:1024 * hf + 1024], T.a[:, 1024 * hf:1024 * hf + 1024]).then_inc(S["la%d" % hf], 16)
    for k in (1, 2, 3):
        load_b(sy, k)

    def quant_b(k):
        p = pair[k]
        v.wait_ge(S["lb%d" % k], 16)
        v.quantize_mx(T.bq[:, CH * p:CH * p + CH], T.bsc[:, CH * p:CH * p + CH],
                      T.b_sb[:, 4 * CH * p:4 * CH * p + 4 * CH]).then_inc(S["bqs%d" % k], 1)

    def bank(k, i):
        b = 512 * (4 * (k % 2) + i)
        return T.ps[:, b:b + CH]

    v.memset(T.g_sb[:], 1.0).then_inc(S.e0, 1)
    quant_b(0)
    for i in range(4):
        if i % 2 == 0:
            v.wait_ge(S["la%d" % (i // 2)], 16)
        v.quantize_mx(T.aq[:, 128 * i:128 * i + 128], T.asc[:, 128 * i:128 * i + 128],
                      T.a_sb[:, 512 * i:512 * i + 512]).then_inc(S["aqs%d" % i], 1)
    for k in range(4):
        v.wait_ge(S["m%d_0" % k], 1)
        v.tensor_copy(T.h[:, 512 * k:512 * k + 512:4], bank(k, 0)).then_inc(S["ev%d" % k], 1)
        if k < 3:
            quant_b(k + 1)
        v.wait_ge(S["ev%d" % k], 4)
        v.quantize_mx(T.hq[:, hcol[k]:hcol[k] + CH], T.hsc[:, hcol[k]:hcol[k] + CH],
                      T.h[:, 512 * k:512 * k + 512]).then_inc(S["hqs%d" % k], 1)
    v.wait_ge(S.e1, 1)
    for t in range(4):
        v.quantize_mx(T.eq[:, 128 * t:128 * t + 128], T.esc[:, 128 * t:128 * t + 128],
                      T.g_sb[:, 4 - t:4 - t + 512]).then_inc(S["pk%d" % t], 1)

    for k in range(4):
        for i in (1, 2, 3):
            s.wait_ge(S["m%d_%d" % (k, i)], 1)
            s.activation(T.h[:, 512 * k + i:512 * k + 512:4], bank(k, i), ActivationFunctionType.Copy).then_inc(S["ev%d" % k], 1)

    for k in range(4):
        p = pair[k]
        te.wait_ge(S["bqs%d" % k], 1)
        if k >= 2:
            te.wait_ge(S["ev%d" % (k - 2)], 4)
        for i in range(4):
            if k == 0:
                te.wait_ge(S["aqs%d" % i], 1)
            te.matmul_mx(bank(k, i), T.aq[:, 128 * i:128 * i + 128], T.asc[:, 128 * i:128 * i + 128],
                         T.bq[:, CH * p:CH * p + CH], T.bsc[:, CH * p:CH * p + CH], True, True).then_inc(S["m%d_%d" % (k, i)], 1)

    g.wait_ge(S.e0, 1)
    g.affine_select(T.g_sb[:], T.g_sb[:], [[-1, 520]], AluOpType.is_equal, 0.0, 4, 4).then_inc(S.e1, 1)
    for k in range(4):
        items = []
        for (tc, dl, eng, straight) in _step(topo, cores, r, k):
            c0 = hcol[k] + PC * (dl[0] % 2)
            if straight:
                lb = _land(r, dl[0], k)
                items.append((tc, ("hq", "hsc"), c0, (lb[0], lb[1]), lb[2], PC, (S["arr%d" % k], S["arr%d" % k]), eng))
            else:
                sl = _slot(k, PLAN[k][dl[0] % 2])
                items.append((tc, ("hq", "hsc"), c0, ("fq", "fsc"), PC * sl, PC, (S["fs%d" % sl], S["fc%d" % sl]), eng))
        g.wait_ge(S["hqs%d" % k], 1)
        for tr in push(items):
            g.remote_dma_fused(tr, local_sem=S.sent)
    g.wait_ge(S.sent, sent[0])

    need = [0, 0, 0, 0]
    for q in range(N):
        for k in range(4):
            for (sc, d, eng) in _last(topo, cores, q, k):
                if d == r:
                    need[k] += 2 * len(eng)
    te.wait_ge(S.ev2, 4)
    for n_, k in enumerate(ORDER[r % 2]):
        te.wait_ge(S["arr%d" % k], need[k])
        if k < 3:
            wq, ws = T.lq[:, CH * k:CH * k + CH], T.lsc[:, CH * k:CH * k + CH]
        else:
            te.wait_ge(S.hqs3, 1)
            w0 = OWN - PC if r % 2 == 0 else OWN + PC
            wq, ws = T.hq[:, w0:w0 + CH], T.hsc[:, w0:w0 + CH]
        for t in range(4):
            if n_ == 0:
                te.wait_ge(S["pk%d" % t], 1)
            mm = te.matmul_mx(T.ps[:, 512 * t:512 * t + CH], T.eq[:, 128 * t:128 * t + 128], T.esc[:, 128 * t:128 * t + 128],
                              wq, ws, n_ == 0, n_ == 3)
            if n_ == 3:
                mm.then_inc(S["d%d" % t], 1)

    for t in (2, 3):
        s.wait_ge(S["d%d" % t], 1)
        s.activation(T.tmp[:, PC * t:PC * t + PC], T.ps[:, 512 * t:512 * t + PC], ActivationFunctionType.Copy).then_inc(S["c%d" % t], 1)
    for t in (0, 1):
        v.wait_ge(S["d%d" % t], 1)
        v.tensor_copy(T.tmp[:, PC * t:PC * t + PC], T.ps[:, 512 * t:512 * t + PC]).then_inc(S["c%d" % t], 1)
    for t in range(4):
        v.wait_ge(S["d%d" % t], 1)
        v.wait_ge(S["c%d" % t], 1)
        v.tensor_tensor(T.y_sb[:, t:256:4], T.ps[:, 512 * t + PC:512 * t + CH], T.tmp[:, PC * t:PC * t + PC], AluOpType.add).then_inc(S.yd, 1)
    sy.wait_ge(S.yd, 4)
    sy.dma_start(T.y[:], T.y_sb[:]).then_inc(S.st, 16)
    sy.wait_ge(S.st, 16)
